import numpy as np
import ml_dtypes

BF16 = ml_dtypes.bfloat16


def bf(x):
    return np.asarray(x, np.float32).astype(BF16)


def f32(x):
    return np.asarray(x, np.float32)


def f64(x):
    return np.asarray(x).astype(np.float64)


def striped(idx):
    return np.concatenate([l.reshape(-1, 16).T for l in idx])


def rows(idx, k):
    return np.tile(np.repeat(idx, 16, axis=0), (k // (16 * 8), 1))


def look(tab, idx):
    return np.take_along_axis(f64(tab), rows(idx, len(tab)), axis=1)


K, S, V, N, M = 512, 2048, 1536, 1536, 512


def setup_inputs():
    return {"tab": f32(np.random.standard_normal((K, S))), "y": f32(np.random.standard_normal((K, V))), "w": bf(np.random.standard_normal((K, M)) / np.sqrt(K)), "b": f32(0.5 * np.random.standard_normal((M, 1))), "offs": striped(np.stack([np.random.permutation(S)[:N] for _ in range(8)]))}


def reference(tab, y, w, b, offs):
    idx = np.stack([g.T.reshape(-1) for g in np.split(offs, 8)])
    t = look(tab, idx)
    x = t**2 * f64(y)
    y = f64(w).T @ x
    return np.maximum(y + f64(b), 0.0)

@@ -1,0 +1,95 @@
+import concourse.mybir as mybir
+
+F32 = mybir.dt.float32
+BF16 = mybir.dt.bfloat16
+U16 = mybir.dt.uint16
+SQUARE = mybir.ActivationFunctionType.Square
+RELU = mybir.ActivationFunctionType.Relu
+ADD = mybir.AluOpType.add
+MAX = mybir.AluOpType.max
+MULT = mybir.AluOpType.mult
+
+P = 128
+R, S = 512, 2048
+N, M = 1536, 512
+C = 512
+ROW_BLOCKS, OUT_BLOCKS = R // P, M // P
+LIST_COLUMNS = C // 16
+FLOPS = 2 * R * M * N
+
+
+def tile_lookup_gate_sq_relu_kernel(tc, tab, y, w, b, offs, out):
+    nc = tc.nc
+    with (
+        tc.tile_pool(name="held", bufs=1) as held,
+        tc.psum_pool(name="psum", bufs=1) as psum,
+    ):
+        offsets = held.tile([P, N // 16], U16, name="offsets")
+        nc.sync.dma_start(offsets[:], offs)
+
+        windows, y_early, y_late = [], [], []
+        weights = held.tile([P, ROW_BLOCKS, M], BF16, name="weights")
+        bias = held.tile([P, OUT_BLOCKS], F32, name="bias")
+        for r in range(ROW_BLOCKS):
+            rows = slice(r * P, (r + 1) * P)
+            window = held.tile([P, S], F32, name=f"window{r}")
+            nc.sync.dma_start(window[:], tab[rows, :])
+            windows.append(window)
+            early = held.tile([P, 2 * C], F32, name=f"y_early{r}")
+            nc.sync.dma_start(early[:], y[rows, : 2 * C])
+            y_early.append(early)
+            if r == 0:
+                nc.sync.dma_start(weights[:], w.rearrange("(r p) m -> p r m", p=P))
+        for r in range(ROW_BLOCKS):
+            late = held.tile([P, C], F32, name=f"y_late{r}")
+            nc.sync.dma_start(late[:], y[r * P : (r + 1) * P, 2 * C :])
+            y_late.append(late)
+        with nc.allow_non_contiguous_dma(reason="the bias: one value a partition for each block"):
+            nc.sync.dma_start(bias[:], b.rearrange("(m p) o -> p (m o)", p=P))
+
+        def gated(r, c):
+            squares = held.tile([P, C], F32, name=f"squares{r}_{c}")
+            piece = offsets[:, c * LIST_COLUMNS : (c + 1) * LIST_COLUMNS]
+            nc.scalar.activation(squares[:], windows[r][:].indirect(piece), SQUARE)
+            stream = y_late[r][:] if c == 2 else y_early[r][:, c * C : (c + 1) * C]
+            x = held.tile([P, C], BF16, name=f"x{r}_{c}")
+            nc.vector.tensor_tensor(x[:], squares[:], stream, MULT)
+            return x
+
+        def add_product(bank, r, m, x):
+            nc.tensor.matmul(
+                bank[:],
+                weights[:, r, m * P : (m + 1) * P],
+                x[:],
+                start=r == 0,
+                stop=r == ROW_BLOCKS - 1,
+            )
+
+        def finish(bank, m, c, on_vector):
+            result = held.tile([P, C], F32, name=f"result{m}_{c}")
+            if on_vector:
+                nc.vector.tensor_scalar(result[:], bank[:], bias[:, m : m + 1], 0.0, ADD, MAX)
+            else:
+                nc.scalar.activation(result[:], bank[:], RELU, bias=bias[:, m : m + 1])
+            nc.sync.dma_start(out[m * P : (m + 1) * P, c * C : (c + 1) * C], result[:])
+
+        banks = [
+            [psum.tile([P, C], F32, name=f"bank{m}_{c}", tag=f"bank{m}_{c}") for m in range(OUT_BLOCKS)]
+            for c in range(2)
+        ]
+        x_late = []
+        for r in range(ROW_BLOCKS):
+            for c in range(2):
+                x = gated(r, c)
+                for m in range(OUT_BLOCKS):
+                    add_product(banks[c][m], r, m, x)
+            x_late.append(gated(r, 2))
+        for c in range(2):
+            for m in range(OUT_BLOCKS):
+                finish(banks[c][m], m, c, on_vector=c == 0)
+
+        for m in range(OUT_BLOCKS):
+            bank = psum.tile([P, C], F32, name=f"bank{m}_2", tag=f"bank{m}_0")
+            for r in range(ROW_BLOCKS):
+                add_product(bank, r, m, x_late[r])
+            finish(bank, m, 2, on_vector=m % 2 == 0)

@@ -27,6 +27,11 @@ def tile_lookup_gate_sq_relu_kernel(tc, tab, y, w, b, offs, out):
         offsets = held.tile([P, N // 16], U16, name="offsets")
         nc.sync.dma_start(offsets[:], offs)
 
+        zeros = held.tile([P, 1], F32, name="zeros")
+        nc.vector.memset(zeros[:], 0.0)
+        unused = held.tile([P, 1], F32, name="unused")
+        nc.scalar.activation(unused[:], zeros[:], SQUARE)
+
         windows, y_early, y_late = [], [], []
         weights = held.tile([P, ROW_BLOCKS, M], BF16, name="weights")
         bias = held.tile([P, OUT_BLOCKS], F32, name="bias")
@@ -35,11 +40,11 @@ def tile_lookup_gate_sq_relu_kernel(tc, tab, y, w, b, offs, out):
             window = held.tile([P, S], F32, name=f"window{r}")
             nc.sync.dma_start(window[:], tab[rows, :])
             windows.append(window)
+            if r == 1:
+                nc.sync.dma_start(weights[:], w.rearrange("(r p) m -> p r m", p=P))
             early = held.tile([P, 2 * C], F32, name=f"y_early{r}")
             nc.sync.dma_start(early[:], y[rows, : 2 * C])
             y_early.append(early)
-            if r == 0:
-                nc.sync.dma_start(weights[:], w.rearrange("(r p) m -> p r m", p=P))
         for r in range(ROW_BLOCKS):
             late = held.tile([P, C], F32, name=f"y_late{r}")
             nc.sync.dma_start(late[:], y[r * P : (r + 1) * P, 2 * C :])
@@ -47,13 +52,15 @@ def tile_lookup_gate_sq_relu_kernel(tc, tab, y, w, b, offs, out):
         with nc.allow_non_contiguous_dma(reason="the bias: one value a partition for each block"):
             nc.sync.dma_start(bias[:], b.rearrange("(m p) o -> p (m o)", p=P))
 
-        def gated(r, c):
+        def look_up(r, c):
             squares = held.tile([P, C], F32, name=f"squares{r}_{c}")
             piece = offsets[:, c * LIST_COLUMNS : (c + 1) * LIST_COLUMNS]
             nc.scalar.activation(squares[:], windows[r][:].indirect(piece), SQUARE)
-            stream = y_late[r][:] if c == 2 else y_early[r][:, c * C : (c + 1) * C]
+            return squares
+
+        def gate(engine, r, c, squares, stream):
             x = held.tile([P, C], BF16, name=f"x{r}_{c}")
-            nc.vector.tensor_tensor(x[:], squares[:], stream, MULT)
+            engine.tensor_tensor(x[:], squares[:], stream, MULT)
             return x
 
         def add_product(bank, r, m, x):
@@ -65,9 +72,9 @@ def tile_lookup_gate_sq_relu_kernel(tc, tab, y, w, b, offs, out):
                 stop=r == ROW_BLOCKS - 1,
             )
 
-        def finish(bank, m, c, on_vector):
+        def finish(bank, m, c):
             result = held.tile([P, C], F32, name=f"result{m}_{c}")
-            if on_vector:
+            if m % 2 == 0:
                 nc.vector.tensor_scalar(result[:], bank[:], bias[:, m : m + 1], 0.0, ADD, MAX)
             else:
                 nc.scalar.activation(result[:], bank[:], RELU, bias=bias[:, m : m + 1])
@@ -77,19 +84,24 @@ def tile_lookup_gate_sq_relu_kernel(tc, tab, y, w, b, offs, out):
             [psum.tile([P, C], F32, name=f"bank{m}_{c}", tag=f"bank{m}_{c}") for m in range(OUT_BLOCKS)]
             for c in range(2)
         ]
-        x_late = []
+        squares_late = []
         for r in range(ROW_BLOCKS):
             for c in range(2):
-                x = gated(r, c)
+                squares = look_up(r, c)
+                x = gate(nc.vector, r, c, squares, y_early[r][:, c * C : (c + 1) * C])
                 for m in range(OUT_BLOCKS):
                     add_product(banks[c][m], r, m, x)
-            x_late.append(gated(r, 2))
+            squares_late.append(look_up(r, 2))
+        x_late = [
+            gate(nc.vector if r % 2 else nc.gpsimd, r, 2, squares_late[r], y_late[r][:])
+            for r in range(ROW_BLOCKS)
+        ]
         for c in range(2):
             for m in range(OUT_BLOCKS):
-                finish(banks[c][m], m, c, on_vector=c == 0)
+                finish(banks[c][m], m, c)
 
         for m in range(OUT_BLOCKS):
             bank = psum.tile([P, C], F32, name=f"bank{m}_2", tag=f"bank{m}_0")
             for r in range(ROW_BLOCKS):
                 add_product(bank, r, m, x_late[r])
-            finish(bank, m, 2, on_vector=m % 2 == 0)
+            finish(bank, m, 2)

@@ -27,21 +27,24 @@ def tile_lookup_gate_sq_relu_kernel(tc, tab, y, w, b, offs, out):
         offsets = held.tile([P, N // 16], U16, name="offsets")
         nc.sync.dma_start(offsets[:], offs)
 
+        bias = held.tile([P, OUT_BLOCKS], F32, name="bias")
+        with nc.allow_non_contiguous_dma(reason="the bias: one value a partition for each block"):
+            nc.gpsimd.dma_start(bias[:], b.rearrange("(m p) o -> p (m o)", p=P))
+
         zeros = held.tile([P, 1], F32, name="zeros")
         nc.vector.memset(zeros[:], 0.0)
         unused = held.tile([P, 1], F32, name="unused")
         nc.scalar.activation(unused[:], zeros[:], SQUARE)
 
-        windows, y_early, y_late = [], [], []
-        weights = held.tile([P, ROW_BLOCKS, M], BF16, name="weights")
-        bias = held.tile([P, OUT_BLOCKS], F32, name="bias")
+        windows, weights, y_early, y_late = [], [], [], []
         for r in range(ROW_BLOCKS):
             rows = slice(r * P, (r + 1) * P)
             window = held.tile([P, S], F32, name=f"window{r}")
             nc.sync.dma_start(window[:], tab[rows, :])
             windows.append(window)
-            if r == 1:
-                nc.sync.dma_start(weights[:], w.rearrange("(r p) m -> p r m", p=P))
+            weight = held.tile([P, M], BF16, name=f"weight{r}")
+            nc.sync.dma_start(weight[:], w[rows, :])
+            weights.append(weight)
             early = held.tile([P, 2 * C], F32, name=f"y_early{r}")
             nc.sync.dma_start(early[:], y[rows, : 2 * C])
             y_early.append(early)
@@ -49,8 +52,6 @@ def tile_lookup_gate_sq_relu_kernel(tc, tab, y, w, b, offs, out):
             late = held.tile([P, C], F32, name=f"y_late{r}")
             nc.sync.dma_start(late[:], y[r * P : (r + 1) * P, 2 * C :])
             y_late.append(late)
-        with nc.allow_non_contiguous_dma(reason="the bias: one value a partition for each block"):
-            nc.sync.dma_start(bias[:], b.rearrange("(m p) o -> p (m o)", p=P))
 
         def look_up(r, c):
             squares = held.tile([P, C], F32, name=f"squares{r}_{c}")
@@ -66,7 +67,7 @@ def tile_lookup_gate_sq_relu_kernel(tc, tab, y, w, b, offs, out):
         def add_product(bank, r, m, x):
             nc.tensor.matmul(
                 bank[:],
-                weights[:, r, m * P : (m + 1) * P],
+                weights[r][:, m * P : (m + 1) * P],
                 x[:],
                 start=r == 0,
                 stop=r == ROW_BLOCKS - 1,
@@ -93,7 +94,7 @@ def tile_lookup_gate_sq_relu_kernel(tc, tab, y, w, b, offs, out):
                     add_product(banks[c][m], r, m, x)
             squares_late.append(look_up(r, 2))
         x_late = [
-            gate(nc.vector if r % 2 else nc.gpsimd, r, 2, squares_late[r], y_late[r][:])
+            gate(nc.vector if r == ROW_BLOCKS - 1 else nc.gpsimd, r, 2, squares_late[r], y_late[r][:])
             for r in range(ROW_BLOCKS)
         ]
         for c in range(2):

@@ -59,9 +59,9 @@ def tile_lookup_gate_sq_relu_kernel(tc, tab, y, w, b, offs, out):
             nc.scalar.activation(squares[:], windows[r][:].indirect(piece), SQUARE)
             return squares
 
-        def gate(engine, r, c, squares, stream):
+        def gate(r, c, squares, stream):
             x = held.tile([P, C], BF16, name=f"x{r}_{c}")
-            engine.tensor_tensor(x[:], squares[:], stream, MULT)
+            nc.vector.tensor_tensor(x[:], squares[:], stream, MULT)
             return x
 
         def add_product(bank, r, m, x):
@@ -89,17 +89,19 @@ def tile_lookup_gate_sq_relu_kernel(tc, tab, y, w, b, offs, out):
         for r in range(ROW_BLOCKS):
             for c in range(2):
                 squares = look_up(r, c)
-                x = gate(nc.vector, r, c, squares, y_early[r][:, c * C : (c + 1) * C])
+                x = gate(r, c, squares, y_early[r][:, c * C : (c + 1) * C])
                 for m in range(OUT_BLOCKS):
                     add_product(banks[c][m], r, m, x)
             squares_late.append(look_up(r, 2))
-        x_late = [
-            gate(nc.vector if r == ROW_BLOCKS - 1 else nc.gpsimd, r, 2, squares_late[r], y_late[r][:])
-            for r in range(ROW_BLOCKS)
-        ]
-        for c in range(2):
-            for m in range(OUT_BLOCKS):
-                finish(banks[c][m], m, c)
+        def gate_late(r):
+            return gate(r, 2, squares_late[r], y_late[r][:])
+
+        x_late = [gate_late(r) for r in range(ROW_BLOCKS - 1)]
+        for m in range(OUT_BLOCKS):
+            finish(banks[0][m], m, 0)
+        x_late.append(gate_late(ROW_BLOCKS - 1))
+        for m in range(OUT_BLOCKS):
+            finish(banks[1][m], m, 1)
 
         for m in range(OUT_BLOCKS):
             bank = psum.tile([P, C], F32, name=f"bank{m}_2", tag=f"bank{m}_0")

import concourse.mybir as mybir

F32 = mybir.dt.float32
BF16 = mybir.dt.bfloat16
U16 = mybir.dt.uint16
SQUARE = mybir.ActivationFunctionType.Square
RELU = mybir.ActivationFunctionType.Relu
ADD = mybir.AluOpType.add
MAX = mybir.AluOpType.max
MULT = mybir.AluOpType.mult

P = 128
R, S = 512, 2048
N, M = 1536, 512
C = 512
ROW_BLOCKS, OUT_BLOCKS = R // P, M // P
LIST_COLUMNS = C // 16
FLOPS = 2 * R * M * N


def tile_lookup_gate_sq_relu_kernel(tc, tab, y, w, b, offs, out):
    nc = tc.nc
    with (
        tc.tile_pool(name="held", bufs=1) as held,
        tc.psum_pool(name="psum", bufs=1) as psum,
    ):
        offsets = held.tile([P, N // 16], U16, name="offsets")
        nc.sync.dma_start(offsets[:], offs)

        bias = held.tile([P, OUT_BLOCKS], F32, name="bias")
        with nc.allow_non_contiguous_dma(reason="the bias: one value a partition for each block"):
            nc.gpsimd.dma_start(bias[:], b.rearrange("(m p) o -> p (m o)", p=P))

        zeros = held.tile([P, 1], F32, name="zeros")
        nc.vector.memset(zeros[:], 0.0)
        unused = held.tile([P, 1], F32, name="unused")
        nc.scalar.activation(unused[:], zeros[:], SQUARE)

        windows, weights, y_early, y_late = [], [], [], []
        for r in range(ROW_BLOCKS):
            rows = slice(r * P, (r + 1) * P)
            window = held.tile([P, S], F32, name=f"window{r}")
            nc.sync.dma_start(window[:], tab[rows, :])
            windows.append(window)
            weight = held.tile([P, M], BF16, name=f"weight{r}")
            nc.sync.dma_start(weight[:], w[rows, :])
            weights.append(weight)
            early = held.tile([P, 2 * C], F32, name=f"y_early{r}")
            nc.sync.dma_start(early[:], y[rows, : 2 * C])
            y_early.append(early)
        for r in range(ROW_BLOCKS):
            late = held.tile([P, C], F32, name=f"y_late{r}")
            nc.sync.dma_start(late[:], y[r * P : (r + 1) * P, 2 * C :])
            y_late.append(late)

        def look_up(r, c):
            squares = held.tile([P, C], F32, name=f"squares{r}_{c}")
            piece = offsets[:, c * LIST_COLUMNS : (c + 1) * LIST_COLUMNS]
            nc.scalar.activation(squares[:], windows[r][:].indirect(piece), SQUARE)
            return squares

        def gate(r, c, squares, stream):
            x = held.tile([P, C], BF16, name=f"x{r}_{c}")
            nc.vector.tensor_tensor(x[:], squares[:], stream, MULT)
            return x

        def add_product(bank, r, m, x):
            nc.tensor.matmul(
                bank[:],
                weights[r][:, m * P : (m + 1) * P],
                x[:],
                start=r == 0,
                stop=r == ROW_BLOCKS - 1,
            )

        def finish(bank, m, c):
            result = held.tile([P, C], F32, name=f"result{m}_{c}")
            if m % 2 == 0:
                nc.vector.tensor_scalar(result[:], bank[:], bias[:, m : m + 1], 0.0, ADD, MAX)
            else:
                nc.scalar.activation(result[:], bank[:], RELU, bias=bias[:, m : m + 1])
            nc.sync.dma_start(out[m * P : (m + 1) * P, c * C : (c + 1) * C], result[:])

        banks = [
            [psum.tile([P, C], F32, name=f"bank{m}_{c}", tag=f"bank{m}_{c}") for m in range(OUT_BLOCKS)]
            for c in range(2)
        ]
        squares_late = []
        for r in range(ROW_BLOCKS):
            for c in range(2):
                squares = look_up(r, c)
                x = gate(r, c, squares, y_early[r][:, c * C : (c + 1) * C])
                for m in range(OUT_BLOCKS):
                    add_product(banks[c][m], r, m, x)
            squares_late.append(look_up(r, 2))
        def gate_late(r):
            return gate(r, 2, squares_late[r], y_late[r][:])

        x_late = [gate_late(r) for r in range(ROW_BLOCKS - 1)]
        for m in range(OUT_BLOCKS):
            finish(banks[0][m], m, 0)
        x_late.append(gate_late(ROW_BLOCKS - 1))
        for m in range(OUT_BLOCKS):
            finish(banks[1][m], m, 1)

        for m in range(OUT_BLOCKS):
            bank = psum.tile([P, C], F32, name=f"bank{m}_2", tag=f"bank{m}_0")
            for r in range(ROW_BLOCKS):
                add_product(bank, r, m, x_late[r])
            finish(bank, m, 2)
